import numpy as np
import ml_dtypes


def mxq(x, axis, fmt="e4m3"):
    dtype, down = {"e4m3": (ml_dtypes.float8_e4m3fn, 7), "e5m2": (ml_dtypes.float8_e5m2, 14)}[fmt]
    v = np.moveaxis(np.asarray(x, np.float32).astype(ml_dtypes.bfloat16).astype(np.float64), axis, -1)
    blocks = v.reshape(v.shape[:-1] + (-1, 32))
    amax = np.abs(blocks).max(-1, keepdims=True)
    byte = np.maximum(np.where(amax > 0, np.frexp(amax)[1] - 1 + 127, 0) - down, 1)
    scale = np.exp2(byte - 127.0)
    codes = (blocks / scale).astype(np.float32).astype(dtype).astype(np.float64)
    return np.moveaxis((codes * scale).reshape(v.shape), -1, axis)


WIDE = False


def mx_kscale(k):
    if not WIDE:
        return np.ones(k)
    levels = np.array([10, -10, 5, -5, 0])
    if k % 512:
        return np.exp2(np.random.permutation(np.resize(levels, k // 32))).repeat(32)
    a = np.empty((k // 512, 16))
    for p in range(k // 512):
        a[p, :8] = np.random.permutation(np.resize(levels, 8))
        for g in range(8):
            far = levels[np.abs(levels - a[p, g]) >= 10]
            a[p, g + 8] = far[np.random.randint(len(far))]
    return np.exp2(a.ravel()).repeat(32)


def f64(x):
    return np.asarray(x).astype(np.float64)


def striped(idx):
    return np.tile(np.asarray(idx).reshape(-1, 16).T, (8, 1)).astype(np.uint16)


def unstriped(offs):
    return offs[:16].T.reshape(-1).astype(np.int64)


E2M1 = np.array([0.0, 0.5, 1.0, 1.5, 2.0, 3.0, 4.0, 6.0, -0.0, -0.5, -1.0, -1.5, -2.0, -3.0, -4.0, -6.0])


def pack_weight(w, fmt):
    k, n = w.shape
    w = f64(np.asarray(w, np.float32).astype(ml_dtypes.bfloat16)).reshape(k // 32, 32, n)
    amax = np.abs(w).max(1)
    if fmt == "e4m3":
        byte = np.frexp(amax)[1] - 1 + 127 - 7
    else:
        mant, ex = np.frexp(amax / 6.0)
        byte = np.where(mant > 0.5, ex, ex - 1) + 127
    byte = np.clip(np.where(amax > 0, byte, 1), 1, 254)
    scaled = (w * np.exp2(127.0 - byte)[:, None, :]).reshape(k, n).astype(np.float32)
    by_word = np.ascontiguousarray(scaled.reshape(k // 512, 128, 4, n).transpose(0, 1, 3, 2))
    if fmt == "e4m3":
        words = by_word.astype(ml_dtypes.float8_e4m3fn).view(np.uint8)
    else:
        c = by_word.astype(ml_dtypes.float4_e2m1fn).view(np.uint8) & 0xF
        words = (c[..., 0::2] | (c[..., 1::2] << 4)).reshape(k // 512, 128, 2 * n)
    return np.ascontiguousarray(words), np.ascontiguousarray(byte.astype(np.uint8).reshape(k // 512, 16, n))


def unpack_weight(words, scales, fmt):
    g, _, n = scales.shape
    words = np.ascontiguousarray(words).reshape(g, 128, n, -1)
    if fmt == "e4m3":
        vals = words.view(ml_dtypes.float8_e4m3fn).astype(np.float64)
    else:
        nib = np.empty((g, 128, n, 4), np.uint8)
        nib[..., 0::2] = words & 0xF
        nib[..., 1::2] = words >> 4
        vals = E2M1[nib]
    vals = vals * np.repeat(np.exp2(scales.astype(np.float64) - 127.0), 8, axis=1)[..., None]
    return vals.transpose(0, 1, 3, 2).reshape(g * 512, n)


D, T, I, Q, E = 512, 2048, 512, 128, 512


def setup_inputs():
    n = np.random.standard_normal
    idx = np.random.permutation(T)[:I]
    fd = mx_kscale(D)
    fi = mx_kscale(I)
    ti = np.ones(T)
    ti[idx] = fi
    keysp = pack_weight(n((D, T)) / fd[:, None], "e4m3")
    return {
        "query": (n((D, Q)) * 0.12 / np.sqrt(D) * fd[:, None]).astype(np.float32),
        "keys_words": keysp[0],
        "keys_scales": keysp[1],
        "kn": np.tile(np.random.uniform(1.5, 2.5, T), (128, 1)).astype(np.float32),
        "qn": (np.random.uniform(1.5, 2.5, (Q, 1))).astype(np.float32),
        "size": (np.random.uniform(0.5, 2.0, (1, I)) * fi).astype(np.float32),
        "vals": (n((E, T)) / ti).astype(np.float32),
        "offs": striped(idx),
    }


def reference(query, keys_words, keys_scales, kn, qn, size, vals, offs):
    idx = unstriped(offs)
    keysu = unpack_weight(keys_words, keys_scales, "e4m3")
    queryq = mxq(f64(query), 0, "e4m3")
    keysidxg = keysu[:, idx]
    a = queryq.T @ keysidxg
    r = 1.0 / (f64(qn) + f64(kn)[:1][:, idx] - 2.0 * a + 0.1)
    w = r * f64(size) / np.sum(r, axis=1, keepdims=True)
    wt = w.T
    vt = f64(vals)[:, idx].T
    wtq = mxq(wt, 0, "e4m3")
    vtq = mxq(vt, 0, "e4m3")
    o = wtq.T @ vtq
    return o

@@ -1,0 +1,185 @@
+from contextlib import ExitStack
+
+import concourse.mybir as mybir
+from concourse.masks import make_identity
+
+D, T, I, Q, E = 512, 2048, 512, 128, 512
+P = 128
+PACK = 4
+BLOCKS = E // P
+
+FLOPS = 2 * Q * I * D + 2 * Q * I * E
+BYTES = 4 * D * Q + D * T + (D // 32) * T + 4 * T + 4 * Q + 4 * I + 4 * E * T + 2 * P * (I // 16) + 4 * Q * E
+
+F32 = mybir.dt.float32
+BF16 = mybir.dt.bfloat16
+I32 = mybir.dt.int32
+U32 = mybir.dt.uint32
+U16 = mybir.dt.uint16
+U8 = mybir.dt.uint8
+FP8X4 = mybir.dt.float8_e4m3fn_x4
+ACT = mybir.ActivationFunctionType
+MULT = mybir.AluOpType.mult
+ADD = mybir.AluOpType.add
+
+
+def tile_attend_necread_kernel(tc, query, keys_words, keys_scales, kn, qn, size, vals, offs, out):
+    nc = tc.nc
+    with ExitStack() as ctx:
+        keep = ctx.enter_context(tc.tile_pool(name="keep", bufs=1))
+        wide = ctx.enter_context(tc.tile_pool(name="wide", bufs=1))
+        psum = ctx.enter_context(tc.psum_pool(name="psum", bufs=1))
+        ring = ctx.enter_context(tc.psum_pool(name="ring", bufs=2))
+
+        offsets = keep.tile([P, I // 16], U16, name="offsets")
+        nc.sync.dma_start(offsets[:], offs)
+
+        ident = keep.tile([P, P], F32, name="ident")
+        make_identity(nc, ident[:])
+        warm = keep.tile([P, 2], F32, name="warm")
+        nc.vector.memset(warm[:, 0:1], 1.0)
+        nc.scalar.activation(warm[:, 1:2], warm[:, 0:1], ACT.Abs_reciprocal_sqrt)
+
+        scale_pool = keep.tile([P, T], U8, name="scale_pool", align_bytes=64)
+        nc.vector.memset(scale_pool[:].bitcast(I32), 0)
+        kn_pool = wide.tile([P, T], F32, name="kn_pool", tag="c")
+        nc.vector.memset(kn_pool[:].bitcast(I32), 0)
+
+        query_raw = wide.tile([P, PACK, Q], F32, name="query_raw", tag="b")
+        nc.sync.dma_start(query_raw[:], query.rearrange("(p j) q -> p j q", j=PACK))
+        word_pool = wide.tile([P, T], I32, name="word_pool", tag="d")
+        nc.sync.dma_start(word_pool[:], keys_words[0].rearrange("p n t -> p (n t)").bitcast(I32))
+        for quad in range(4):
+            nc.scalar.dma_start(
+                scale_pool[32 * quad : 32 * quad + 4, :].bitcast(I32),
+                keys_scales[0, 4 * quad : 4 * quad + 4, :].bitcast(I32),
+            )
+        nc.scalar.dma_start(kn_pool[0:1, :], kn[0:1, :])
+
+        qn_col = keep.tile([P, 1], F32, name="qn_col")
+        nc.gpsimd.dma_start(qn_col[:], qn)
+        size_cols = keep.tile([P, PACK], F32, name="size_cols")
+        nc.gpsimd.dma_start(size_cols[:], size.rearrange("o (p t) -> (o p) t", t=PACK))
+        row_bias = keep.tile([P, 1], F32, name="row_bias")
+        nc.gpsimd.tensor_scalar(row_bias[:], qn_col[:], 1.0, 0.1, MULT, ADD)
+
+
+        def load_vals(c, tag):
+            pool_c = wide.tile([P, T], F32, name=f"vals{c}", tag=tag)
+            nc.sync.dma_start(pool_c[:], vals[c * P : (c + 1) * P, :])
+            return pool_c
+
+        def quantize(grouped, name):
+            codes = keep.tile([P, P], U32, name=name + "_codes", align_bytes=64)
+            scales = keep.tile([P, P], U8, name=name + "_scales", align_bytes=64)
+            nc.vector.quantize_mx(out=codes[:].bitcast(FP8X4), scales=scales[:], in_=grouped)
+            return codes, scales
+
+        def turn_slots(rows, name, bank):
+            words = rows[:].bitcast(F32)
+            for u in range(2):
+                nc.tensor.transpose(bank[:, u, :], words[:, u : I // 2 : 2], ident[:])
+            grouped = keep.tile([P, P * PACK], BF16, name=name + "_grouped", align_bytes=64)
+            nc.scalar.copy(
+                grouped[:].bitcast(F32).rearrange("p (r u) -> p r u", u=2),
+                bank[:].rearrange("p u r -> p r u"),
+            )
+            return quantize(grouped[:], name)
+
+        vals_pools = [load_vals(0, "a")]
+
+        key_scales = keep.tile([P, I], U8, name="key_scales", align_bytes=64)
+        nc.vector.tensor_copy(key_scales[:], scale_pool[:].indirect(offsets[:]))
+        kn_listed = keep.tile([P, I], F32, name="kn_listed", tag="listed0", align_bytes=64)
+        nc.vector.tensor_copy(kn_listed[:], kn_pool[:].indirect(offsets[:]))
+
+        query_grouped = keep.tile([P, Q, PACK], BF16, name="query_grouped", align_bytes=64)
+        nc.vector.tensor_copy(query_grouped[:], query_raw[:].rearrange("p j q -> p q j"))
+        q_codes, q_scales = quantize(query_grouped[:].rearrange("p q j -> p (q j)"), "query")
+        vals_pools.append(load_vals(1, "b"))
+
+        key_words = keep.tile([P, I], U32, name="key_words", align_bytes=64)
+        nc.vector.tensor_copy(key_words[:], word_pool[:].bitcast(U32).indirect(offsets[:]))
+        vals_pools.append(load_vals(2, "c"))
+        vals_pools.append(load_vals(3, "d"))
+
+        kn_turned = psum.tile([P, PACK, P], F32, name="kn_turned", tag="turn")
+        for j in range(PACK):
+            nc.tensor.transpose(kn_turned[:, j, :], kn_listed[:, j * P : (j + 1) * P], ident[:])
+        kn_cols = keep.tile([P, PACK], F32, name="kn_cols")
+        nc.scalar.copy(kn_cols[:], kn_turned[:, :, 0])
+
+        size_rows = psum.tile([P, PACK, P], F32, name="size_rows")
+        for t in range(PACK):
+            nc.tensor.transpose(size_rows[:, t, :], size_cols[:, t : t + 1].to_broadcast([P, P]), ident[:])
+
+        scores = psum.tile([P, PACK, Q], F32, name="scores")
+        for j in range(PACK):
+            nc.tensor.matmul_mx(
+                out=scores[:, j, :],
+                lhsT=key_words[:, j * P : (j + 1) * P].bitcast(FP8X4),
+                lhsT_scale=key_scales[:, j * P : (j + 1) * P],
+                rhs=q_codes[:].bitcast(FP8X4),
+                rhs_scale=q_scales[:],
+                start=True,
+                stop=True,
+            )
+        part = keep.tile([P, PACK, Q], F32, name="part")
+        for j in range(PACK):
+            nc.scalar.activation(part[:, j, :], scores[:, j, :], ACT.Identity, bias=kn_cols[:, j : j + 1], scale=-2.0)
+        part_rows = psum.tile([P, I], F32, name="part_rows")
+        for j in range(PACK):
+            nc.tensor.transpose(part_rows[:, j * P : (j + 1) * P], part[:, j, :], ident[:])
+
+        root = keep.tile([P, I], F32, name="root")
+        nc.scalar.activation(root[:], part_rows[:], ACT.Abs_reciprocal_sqrt, bias=row_bias[:])
+        signs = keep.tile([P, I], F32, name="signs")
+        nc.scalar.activation(signs[:], part_rows[:], ACT.Sign, bias=row_bias[:])
+        magnitude = keep.tile([P, I], F32, name="magnitude")
+        nc.scalar.activation(magnitude[:], root[:], ACT.Square)
+
+        def gather_vals(c):
+            listed = keep.tile([P, I], BF16, name=f"listed{c}", align_bytes=64)
+            nc.vector.tensor_copy(listed[:], vals_pools[c][:].indirect(offsets[:]))
+            bank = ring.tile([P, 2, P], F32, name="vals_turned")
+            return turn_slots(listed, f"vals{c}", bank)
+
+        v_ops = [gather_vals(0)]
+
+        recip = keep.tile([P, I], F32, name="recip")
+        row_sum = keep.tile([P, 1], F32, name="row_sum")
+        nc.vector.scalar_tensor_tensor(recip[:], magnitude[:], 1.0, signs[:], MULT, MULT, accum_out=row_sum[:])
+        inv_sum = keep.tile([P, 1], F32, name="inv_sum")
+        nc.vector.reciprocal(inv_sum[:], row_sum[:])
+        weights = keep.tile([P, I], BF16, name="weights", align_bytes=64)
+        nc.vector.scalar_tensor_tensor(
+            weights[:].rearrange("q (s t) -> q s t", t=PACK),
+            recip[:].rearrange("q (s t) -> q s t", t=PACK),
+            inv_sum[:],
+            size_rows[:].rearrange("q t s -> q s t"),
+            MULT,
+            MULT,
+        )
+        weights_turned = psum.tile([P, 2, P], F32, name="weights_turned", tag="turn")
+        w_codes, w_scales = turn_slots(weights, "weights", weights_turned)
+
+        for c in range(1, BLOCKS):
+            v_ops.append(gather_vals(c))
+
+        for first, last in ((0, BLOCKS - 1), (BLOCKS - 1, BLOCKS)):
+            width = (last - first) * P
+            acc = psum.tile([P, width], F32, name=f"acc{first}")
+            for c in range(first, last):
+                v_codes, v_scales = v_ops[c]
+                nc.tensor.matmul_mx(
+                    out=acc[:, (c - first) * P : (c - first + 1) * P],
+                    lhsT=w_codes[:].bitcast(FP8X4),
+                    lhsT_scale=w_scales[:],
+                    rhs=v_codes[:].bitcast(FP8X4),
+                    rhs_scale=v_scales[:],
+                    start=True,
+                    stop=True,
+                )
+            result = keep.tile([P, width], F32, name=f"result{first}")
+            nc.scalar.copy(result[:], acc[:])
+            nc.sync.dma_start(out[:, first * P : last * P], result[:])

@@ -6,7 +6,6 @@ from concourse.masks import make_identity
 D, T, I, Q, E = 512, 2048, 512, 128, 512
 P = 128
 PACK = 4
-BLOCKS = E // P
 
 FLOPS = 2 * Q * I * D + 2 * Q * I * E
 BYTES = 4 * D * Q + D * T + (D // 32) * T + 4 * T + 4 * Q + 4 * I + 4 * E * T + 2 * P * (I // 16) + 4 * Q * E
@@ -26,132 +25,142 @@ ADD = mybir.AluOpType.add
 def tile_attend_necread_kernel(tc, query, keys_words, keys_scales, kn, qn, size, vals, offs, out):
     nc = tc.nc
     with ExitStack() as ctx:
-        keep = ctx.enter_context(tc.tile_pool(name="keep", bufs=1))
-        wide = ctx.enter_context(tc.tile_pool(name="wide", bufs=1))
+        sbuf = ctx.enter_context(tc.tile_pool(name="sbuf", bufs=1))
         psum = ctx.enter_context(tc.psum_pool(name="psum", bufs=1))
-        ring = ctx.enter_context(tc.psum_pool(name="ring", bufs=2))
 
-        offsets = keep.tile([P, I // 16], U16, name="offsets")
+        def tile(name, columns, dtype, after=None):
+            return sbuf.tile([P, columns], dtype, name=name, tag=after or name, align_bytes=64)
+
+        offsets = tile("offsets", I // 16, U16)
         nc.sync.dma_start(offsets[:], offs)
 
-        ident = keep.tile([P, P], F32, name="ident")
-        make_identity(nc, ident[:])
-        warm = keep.tile([P, 2], F32, name="warm")
-        nc.vector.memset(warm[:, 0:1], 1.0)
-        nc.scalar.activation(warm[:, 1:2], warm[:, 0:1], ACT.Abs_reciprocal_sqrt)
-
-        scale_pool = keep.tile([P, T], U8, name="scale_pool", align_bytes=64)
-        nc.vector.memset(scale_pool[:].bitcast(I32), 0)
-        kn_pool = wide.tile([P, T], F32, name="kn_pool", tag="c")
+        scale_pool = tile("scale_pool", T, U8)
+        nc.gpsimd.memset(scale_pool[:].bitcast(I32), 0)
+        kn_pool = tile("kn_pool", T, F32)
         nc.vector.memset(kn_pool[:].bitcast(I32), 0)
 
-        query_raw = wide.tile([P, PACK, Q], F32, name="query_raw", tag="b")
-        nc.sync.dma_start(query_raw[:], query.rearrange("(p j) q -> p j q", j=PACK))
-        word_pool = wide.tile([P, T], I32, name="word_pool", tag="d")
+        query_raw = tile("query_raw", PACK * Q, F32)
+        nc.sync.dma_start(query_raw[:], query.rearrange("(p j) q -> p (j q)", j=PACK))
+        word_pool = tile("word_pool", T, I32)
         nc.sync.dma_start(word_pool[:], keys_words[0].rearrange("p n t -> p (n t)").bitcast(I32))
+        qn_col = tile("qn_col", 1, F32)
+        nc.gpsimd.dma_start(qn_col[:], qn)
+        size_cols = tile("size_cols", PACK, F32)
+        nc.gpsimd.dma_start(size_cols[:], size.rearrange("o (p t) -> (o p) t", t=PACK))
         for quad in range(4):
             nc.scalar.dma_start(
                 scale_pool[32 * quad : 32 * quad + 4, :].bitcast(I32),
                 keys_scales[0, 4 * quad : 4 * quad + 4, :].bitcast(I32),
             )
         nc.scalar.dma_start(kn_pool[0:1, :], kn[0:1, :])
+        warm = tile("warm", 1, F32)
+        nc.scalar.activation(warm[64:128, :], kn_pool[64:128, 0:1], ACT.Abs_reciprocal_sqrt, bias=1.0)
 
-        qn_col = keep.tile([P, 1], F32, name="qn_col")
-        nc.gpsimd.dma_start(qn_col[:], qn)
-        size_cols = keep.tile([P, PACK], F32, name="size_cols")
-        nc.gpsimd.dma_start(size_cols[:], size.rearrange("o (p t) -> (o p) t", t=PACK))
-        row_bias = keep.tile([P, 1], F32, name="row_bias")
+        ident = tile("ident", P, F32)
+        make_identity(nc, ident[:])
+        row_bias = tile("row_bias", 1, F32)
         nc.gpsimd.tensor_scalar(row_bias[:], qn_col[:], 1.0, 0.1, MULT, ADD)
 
-
-        def load_vals(c, tag):
-            pool_c = wide.tile([P, T], F32, name=f"vals{c}", tag=tag)
+        def load_vals(c, after):
+            pool_c = tile(f"vals{c}", T, F32, after)
             nc.sync.dma_start(pool_c[:], vals[c * P : (c + 1) * P, :])
             return pool_c
 
-        def quantize(grouped, name):
-            codes = keep.tile([P, P], U32, name=name + "_codes", align_bytes=64)
-            scales = keep.tile([P, P], U8, name=name + "_scales", align_bytes=64)
-            nc.vector.quantize_mx(out=codes[:].bitcast(FP8X4), scales=scales[:], in_=grouped)
+        def quantize(grouped, name, words, after=None):
+            codes = tile(name + "_codes", words, U32, after)
+            scales = tile(name + "_scales", words, U8)
+            nc.vector.quantize_mx(out=codes[:].bitcast(FP8X4), scales=scales[:], in_=grouped[:])
             return codes, scales
 
-        def turn_slots(rows, name, bank):
+        def multiply(acc, lhs, lhs_first, rhs, rhs_first, columns):
+            nc.tensor.matmul_mx(
+                out=acc,
+                lhsT=lhs[0][:, lhs_first : lhs_first + P].bitcast(FP8X4),
+                lhsT_scale=lhs[1][:, lhs_first : lhs_first + P],
+                rhs=rhs[0][:, rhs_first : rhs_first + columns].bitcast(FP8X4),
+                rhs_scale=rhs[1][:, rhs_first : rhs_first + columns],
+                start=True,
+                stop=True,
+            )
+
+        def turn(rows, bank):
             words = rows[:].bitcast(F32)
             for u in range(2):
                 nc.tensor.transpose(bank[:, u, :], words[:, u : I // 2 : 2], ident[:])
-            grouped = keep.tile([P, P * PACK], BF16, name=name + "_grouped", align_bytes=64)
+
+        def interleave(grouped, bank):
             nc.scalar.copy(
-                grouped[:].bitcast(F32).rearrange("p (r u) -> p r u", u=2),
-                bank[:].rearrange("p u r -> p r u"),
+                grouped.bitcast(F32).rearrange("p (c r u) -> p c r u", r=P, u=2),
+                bank[:].rearrange("p c u r -> p c r u"),
             )
-            return quantize(grouped[:], name)
 
-        vals_pools = [load_vals(0, "a")]
+        def gather_vals(c, bank, after=None):
+            listed = tile(f"listed{c}", I, BF16, after)
+            nc.vector.tensor_copy(listed[:], vals_pools[c][:].indirect(offsets[:]))
+            turn(listed, bank)
 
-        key_scales = keep.tile([P, I], U8, name="key_scales", align_bytes=64)
+        query_grouped = tile("query_grouped", Q * PACK, BF16)
+        nc.vector.tensor_copy(
+            query_grouped[:].rearrange("p (q j) -> p q j", j=PACK),
+            query_raw[:].rearrange("p (j q) -> p q j", j=PACK),
+        )
+        query_mx = quantize(query_grouped, "query", Q)
+
+        key_scales = tile("key_scales", I, U8)
         nc.vector.tensor_copy(key_scales[:], scale_pool[:].indirect(offsets[:]))
-        kn_listed = keep.tile([P, I], F32, name="kn_listed", tag="listed0", align_bytes=64)
+        kn_listed = tile("kn_listed", I, F32, "scale_pool")
         nc.vector.tensor_copy(kn_listed[:], kn_pool[:].indirect(offsets[:]))
-
-        query_grouped = keep.tile([P, Q, PACK], BF16, name="query_grouped", align_bytes=64)
-        nc.vector.tensor_copy(query_grouped[:], query_raw[:].rearrange("p j q -> p q j"))
-        q_codes, q_scales = quantize(query_grouped[:].rearrange("p q j -> p (q j)"), "query")
-        vals_pools.append(load_vals(1, "b"))
-
-        key_words = keep.tile([P, I], U32, name="key_words", align_bytes=64)
+        key_words = tile("key_words", I, U32, "kn_pool")
         nc.vector.tensor_copy(key_words[:], word_pool[:].bitcast(U32).indirect(offsets[:]))
-        vals_pools.append(load_vals(2, "c"))
-        vals_pools.append(load_vals(3, "d"))
+
+        vals_pools = [
+            load_vals(c, after) for c, after in enumerate(("query_raw", "query_grouped", "warm", "word_pool"))
+        ]
 
         kn_turned = psum.tile([P, PACK, P], F32, name="kn_turned", tag="turn")
         for j in range(PACK):
             nc.tensor.transpose(kn_turned[:, j, :], kn_listed[:, j * P : (j + 1) * P], ident[:])
-        kn_cols = keep.tile([P, PACK], F32, name="kn_cols")
+        kn_cols = tile("kn_cols", PACK, F32)
         nc.scalar.copy(kn_cols[:], kn_turned[:, :, 0])
 
-        size_rows = psum.tile([P, PACK, P], F32, name="size_rows")
+        scores = psum.tile([P, PACK, Q], F32, name="scores", tag="turn")
+        for j in range(PACK):
+            multiply(scores[:, j, :], (key_words, key_scales), j * P, query_mx, 0, Q)
+        part = tile("part", PACK * Q, F32)
+        part_rows = psum.tile([P, I], F32, name="part_rows")
+        for j in range(PACK):
+            cols = slice(j * P, (j + 1) * P)
+            nc.scalar.activation(part[:, cols], scores[:, j, :], ACT.Identity, bias=kn_cols[:, j : j + 1], scale=-2.0)
+            nc.tensor.transpose(part_rows[:, cols], part[:, cols], ident[:])
+
+        root = tile("root", I, F32)
+        nc.scalar.activation(root[:], part_rows[:], ACT.Abs_reciprocal_sqrt, bias=row_bias[:])
+        signs = tile("signs", I, F32)
+        nc.scalar.activation(signs[:], part_rows[:], ACT.Sign, bias=row_bias[:])
+        magnitude = tile("magnitude", I, F32)
+        nc.scalar.activation(magnitude[:], root[:], ACT.Square)
+
+        size_rows = psum.tile([P, PACK, P], F32, name="size_rows", tag="part_rows")
         for t in range(PACK):
             nc.tensor.transpose(size_rows[:, t, :], size_cols[:, t : t + 1].to_broadcast([P, P]), ident[:])
 
-        scores = psum.tile([P, PACK, Q], F32, name="scores")
-        for j in range(PACK):
-            nc.tensor.matmul_mx(
-                out=scores[:, j, :],
-                lhsT=key_words[:, j * P : (j + 1) * P].bitcast(FP8X4),
-                lhsT_scale=key_scales[:, j * P : (j + 1) * P],
-                rhs=q_codes[:].bitcast(FP8X4),
-                rhs_scale=q_scales[:],
-                start=True,
-                stop=True,
-            )
-        part = keep.tile([P, PACK, Q], F32, name="part")
-        for j in range(PACK):
-            nc.scalar.activation(part[:, j, :], scores[:, j, :], ACT.Identity, bias=kn_cols[:, j : j + 1], scale=-2.0)
-        part_rows = psum.tile([P, I], F32, name="part_rows")
-        for j in range(PACK):
-            nc.tensor.transpose(part_rows[:, j * P : (j + 1) * P], part[:, j, :], ident[:])
+        early = tile("early", 2 * I, BF16, "root")
+        early_turned = psum.tile([P, 2, 2, P], F32, name="early_turned", tag="turn")
+        for c in range(2):
+            gather_vals(c, early_turned[:, c])
+        interleave(early[:], early_turned)
+        late = tile("late", 2 * I, BF16)
+        third_turned = psum.tile([P, 1, 2, P], F32, name="third_turned")
+        gather_vals(2, third_turned[:, 0])
+        interleave(late[:, I : 2 * I], third_turned)
 
-        root = keep.tile([P, I], F32, name="root")
-        nc.scalar.activation(root[:], part_rows[:], ACT.Abs_reciprocal_sqrt, bias=row_bias[:])
-        signs = keep.tile([P, I], F32, name="signs")
-        nc.scalar.activation(signs[:], part_rows[:], ACT.Sign, bias=row_bias[:])
-        magnitude = keep.tile([P, I], F32, name="magnitude")
-        nc.scalar.activation(magnitude[:], root[:], ACT.Square)
-
-        def gather_vals(c):
-            listed = keep.tile([P, I], BF16, name=f"listed{c}", align_bytes=64)
-            nc.vector.tensor_copy(listed[:], vals_pools[c][:].indirect(offsets[:]))
-            bank = ring.tile([P, 2, P], F32, name="vals_turned")
-            return turn_slots(listed, f"vals{c}", bank)
-
-        v_ops = [gather_vals(0)]
-
-        recip = keep.tile([P, I], F32, name="recip")
-        row_sum = keep.tile([P, 1], F32, name="row_sum")
+        recip = tile("recip", I, F32, "warm")
+        row_sum = tile("row_sum", 1, F32)
         nc.vector.scalar_tensor_tensor(recip[:], magnitude[:], 1.0, signs[:], MULT, MULT, accum_out=row_sum[:])
-        inv_sum = keep.tile([P, 1], F32, name="inv_sum")
+        early_mx = quantize(early, "early", 2 * P, "signs")
+        inv_sum = tile("inv_sum", 1, F32)
         nc.vector.reciprocal(inv_sum[:], row_sum[:])
-        weights = keep.tile([P, I], BF16, name="weights", align_bytes=64)
+        weights = tile("weights", I, BF16)
         nc.vector.scalar_tensor_tensor(
             weights[:].rearrange("q (s t) -> q s t", t=PACK),
             recip[:].rearrange("q (s t) -> q s t", t=PACK),
@@ -160,26 +169,26 @@ def tile_attend_necread_kernel(tc, query, keys_words, keys_scales, kn, qn, size,
             MULT,
             MULT,
         )
-        weights_turned = psum.tile([P, 2, P], F32, name="weights_turned", tag="turn")
-        w_codes, w_scales = turn_slots(weights, "weights", weights_turned)
+        weights_turned = psum.tile([P, 1, 2, P], F32, name="weights_turned")
+        turn(weights, weights_turned[:, 0])
+        interleave(late[:, 0:I], weights_turned)
 
-        for c in range(1, BLOCKS):
-            v_ops.append(gather_vals(c))
+        last = tile("last", I, BF16)
+        last_turned = psum.tile([P, 1, 2, P], F32, name="last_turned")
+        gather_vals(3, last_turned[:, 0], "warm")
+        interleave(last[:], last_turned)
+        late_mx = quantize(late, "late", 2 * P, "word_pool")
+        last_mx = quantize(last, "last", P)
 
-        for first, last in ((0, BLOCKS - 1), (BLOCKS - 1, BLOCKS)):
-            width = (last - first) * P
-            acc = psum.tile([P, width], F32, name=f"acc{first}")
-            for c in range(first, last):
-                v_codes, v_scales = v_ops[c]
-                nc.tensor.matmul_mx(
-                    out=acc[:, (c - first) * P : (c - first + 1) * P],
-                    lhsT=w_codes[:].bitcast(FP8X4),
-                    lhsT_scale=w_scales[:],
-                    rhs=v_codes[:].bitcast(FP8X4),
-                    rhs_scale=v_scales[:],
-                    start=True,
-                    stop=True,
-                )
-            result = keep.tile([P, width], F32, name=f"result{first}")
-            nc.scalar.copy(result[:], acc[:])
-            nc.sync.dma_start(out[:, first * P : last * P], result[:])
+        acc = psum.tile([P, 3 * P], F32, name="acc")
+        multiply(acc[:, 0 : 2 * P], late_mx, 0, early_mx, 0, 2 * P)
+        multiply(acc[:, 2 * P : 3 * P], late_mx, 0, late_mx, P, P)
+        result = tile("result", 3 * P, F32)
+        nc.scalar.copy(result[:], acc[:])
+        nc.sync.dma_start(out[:, 0 : 3 * P], result[:])
+
+        acc_last = psum.tile([P, P], F32, name="acc_last", tag="part_rows")
+        multiply(acc_last[:], late_mx, 0, last_mx, 0, P)
+        result_last = tile("result_last", P, F32)
+        nc.scalar.copy(result_last[:], acc_last[:])
+        nc.scalar.dma_start(out[:, 3 * P : E], result_last[:])

@@ -1,11 +1,12 @@
 from contextlib import ExitStack
 
 import concourse.mybir as mybir
-from concourse.masks import make_identity
 
 D, T, I, Q, E = 512, 2048, 512, 128, 512
 P = 128
 PACK = 4
+HALF = I // 2
+KN_SPLIT = 1408
 
 FLOPS = 2 * Q * I * D + 2 * Q * I * E
 BYTES = 4 * D * Q + D * T + (D // 32) * T + 4 * T + 4 * Q + 4 * I + 4 * E * T + 2 * P * (I // 16) + 4 * Q * E
@@ -20,6 +21,9 @@ FP8X4 = mybir.dt.float8_e4m3fn_x4
 ACT = mybir.ActivationFunctionType
 MULT = mybir.AluOpType.mult
 ADD = mybir.AluOpType.add
+SUBTRACT = mybir.AluOpType.subtract
+IS_EQUAL = mybir.AluOpType.is_equal
+IS_GE = mybir.AluOpType.is_ge
 
 
 def tile_attend_necread_kernel(tc, query, keys_words, keys_scales, kn, qn, size, vals, offs, out):
@@ -37,27 +41,31 @@ def tile_attend_necread_kernel(tc, query, keys_words, keys_scales, kn, qn, size,
         scale_pool = tile("scale_pool", T, U8)
         nc.gpsimd.memset(scale_pool[:].bitcast(I32), 0)
         kn_pool = tile("kn_pool", T, F32)
-        nc.vector.memset(kn_pool[:].bitcast(I32), 0)
+        nc.vector.memset(kn_pool[:, 0:KN_SPLIT].bitcast(I32), 0)
+        nc.gpsimd.memset(kn_pool[:, KN_SPLIT:T].bitcast(I32), 0)
 
-        query_raw = tile("query_raw", PACK * Q, F32)
-        nc.sync.dma_start(query_raw[:], query.rearrange("(p j) q -> p (j q)", j=PACK))
+        diagonal = tile("diagonal", P, I32)
+        nc.gpsimd.iota(diagonal[:], [[1, P]], base=0, channel_multiplier=-1)
+        ident = tile("ident", P, F32)
+        nc.vector.tensor_scalar(ident[:], diagonal[:], 0.0, None, IS_EQUAL)
+
         word_pool = tile("word_pool", T, I32)
         nc.sync.dma_start(word_pool[:], keys_words[0].rearrange("p n t -> p (n t)").bitcast(I32))
+        query_raw = tile("query_raw", PACK * Q, F32)
+        nc.sync.dma_start(query_raw[:], query.rearrange("(p j) q -> p (j q)", j=PACK))
         qn_col = tile("qn_col", 1, F32)
         nc.gpsimd.dma_start(qn_col[:], qn)
         size_cols = tile("size_cols", PACK, F32)
         nc.gpsimd.dma_start(size_cols[:], size.rearrange("o (p t) -> (o p) t", t=PACK))
         for quad in range(4):
-            nc.scalar.dma_start(
+            nc.sync.dma_start(
                 scale_pool[32 * quad : 32 * quad + 4, :].bitcast(I32),
                 keys_scales[0, 4 * quad : 4 * quad + 4, :].bitcast(I32),
             )
-        nc.scalar.dma_start(kn_pool[0:1, :], kn[0:1, :])
-        warm = tile("warm", 1, F32)
-        nc.scalar.activation(warm[64:128, :], kn_pool[64:128, 0:1], ACT.Abs_reciprocal_sqrt, bias=1.0)
+        nc.sync.dma_start(kn_pool[0:1, :], kn[0:1, :])
+        warm = tile("warm", 2, F32)
+        nc.scalar.activation(warm[64:128, :], kn_pool[64:128, KN_SPLIT - 1 : KN_SPLIT + 1], ACT.Abs_reciprocal_sqrt, bias=1.0)
 
-        ident = tile("ident", P, F32)
-        make_identity(nc, ident[:])
         row_bias = tile("row_bias", 1, F32)
         nc.gpsimd.tensor_scalar(row_bias[:], qn_col[:], 1.0, 0.1, MULT, ADD)
 
@@ -100,21 +108,24 @@ def tile_attend_necread_kernel(tc, query, keys_words, keys_scales, kn, qn, size,
             turn(listed, bank)
 
         query_grouped = tile("query_grouped", Q * PACK, BF16)
-        nc.vector.tensor_copy(
+        nc.scalar.copy(
             query_grouped[:].rearrange("p (q j) -> p q j", j=PACK),
             query_raw[:].rearrange("p (j q) -> p q j", j=PACK),
         )
-        query_mx = quantize(query_grouped, "query", Q)
-
-        key_scales = tile("key_scales", I, U8)
-        nc.vector.tensor_copy(key_scales[:], scale_pool[:].indirect(offsets[:]))
-        kn_listed = tile("kn_listed", I, F32, "scale_pool")
-        nc.vector.tensor_copy(kn_listed[:], kn_pool[:].indirect(offsets[:]))
-        key_words = tile("key_words", I, U32, "kn_pool")
+        key_words = tile("key_words", I, U32)
         nc.vector.tensor_copy(key_words[:], word_pool[:].bitcast(U32).indirect(offsets[:]))
+        kn_listed = tile("kn_listed", I, F32, "word_pool")
+        nc.vector.tensor_copy(kn_listed[:], kn_pool[:].indirect(offsets[:]))
+        key_scales = tile("key_scales", I, U8, "kn_pool")
+        query_mx = quantize(query_grouped, "query", Q)
+        for h in range(2):
+            nc.vector.tensor_copy(
+                key_scales[:, h * HALF : (h + 1) * HALF],
+                scale_pool[:].indirect(offsets[:, h * HALF // 16 : (h + 1) * HALF // 16]),
+            )
 
         vals_pools = [
-            load_vals(c, after) for c, after in enumerate(("query_raw", "query_grouped", "warm", "word_pool"))
+            load_vals(c, after) for c, after in enumerate(("diagonal", "warm", "query_raw", "query_grouped"))
         ]
 
         kn_turned = psum.tile([P, PACK, P], F32, name="kn_turned", tag="turn")
@@ -123,41 +134,48 @@ def tile_attend_necread_kernel(tc, query, keys_words, keys_scales, kn, qn, size,
         kn_cols = tile("kn_cols", PACK, F32)
         nc.scalar.copy(kn_cols[:], kn_turned[:, :, 0])
 
-        scores = psum.tile([P, PACK, Q], F32, name="scores", tag="turn")
-        for j in range(PACK):
-            multiply(scores[:, j, :], (key_words, key_scales), j * P, query_mx, 0, Q)
         part = tile("part", PACK * Q, F32)
-        part_rows = psum.tile([P, I], F32, name="part_rows")
-        for j in range(PACK):
-            cols = slice(j * P, (j + 1) * P)
-            nc.scalar.activation(part[:, cols], scores[:, j, :], ACT.Identity, bias=kn_cols[:, j : j + 1], scale=-2.0)
-            nc.tensor.transpose(part_rows[:, cols], part[:, cols], ident[:])
+        part_rows = []
+        for h in range(2):
+            scores = psum.tile([P, 2, Q], F32, name=f"scores{h}")
+            for jj in range(2):
+                multiply(scores[:, jj, :], (key_words, key_scales), (2 * h + jj) * P, query_mx, 0, Q)
+            part_rows.append(psum.tile([P, HALF], F32, name=f"part_rows{h}"))
+            for jj in range(2):
+                j = 2 * h + jj
+                cols = slice(j * P, (j + 1) * P)
+                nc.scalar.activation(
+                    part[:, cols], scores[:, jj, :], ACT.Identity, bias=kn_cols[:, j : j + 1], scale=-2.0
+                )
+                nc.tensor.transpose(part_rows[h][:, jj * P : (jj + 1) * P], part[:, cols], ident[:])
 
         root = tile("root", I, F32)
-        nc.scalar.activation(root[:], part_rows[:], ACT.Abs_reciprocal_sqrt, bias=row_bias[:])
-        signs = tile("signs", I, F32)
-        nc.scalar.activation(signs[:], part_rows[:], ACT.Sign, bias=row_bias[:])
         magnitude = tile("magnitude", I, F32)
-        nc.scalar.activation(magnitude[:], root[:], ACT.Square)
+        for h in range(2):
+            cols = slice(h * HALF, (h + 1) * HALF)
+            nc.scalar.activation(root[:, cols], part_rows[h][:], ACT.Abs_reciprocal_sqrt, bias=row_bias[:])
+            nc.scalar.activation(magnitude[:, cols], root[:, cols], ACT.Square)
 
-        size_rows = psum.tile([P, PACK, P], F32, name="size_rows", tag="part_rows")
+        early_turned = psum.tile([P, 2, 2, P], F32, name="early_turned", tag="scores1")
+        for c in range(2):
+            gather_vals(c, early_turned[:, c])
+        positive = tile("positive", I, F32, "warm")
+        for h in range(2):
+            nc.vector.tensor_scalar(
+                positive[:, h * HALF : (h + 1) * HALF], part_rows[h][:], row_bias[:], 0.0, ADD, IS_GE
+            )
+
+        size_rows = psum.tile([P, PACK, P], F32, name="size_rows", tag="part_rows0")
         for t in range(PACK):
             nc.tensor.transpose(size_rows[:, t, :], size_cols[:, t : t + 1].to_broadcast([P, P]), ident[:])
 
         early = tile("early", 2 * I, BF16, "root")
-        early_turned = psum.tile([P, 2, 2, P], F32, name="early_turned", tag="turn")
-        for c in range(2):
-            gather_vals(c, early_turned[:, c])
         interleave(early[:], early_turned)
-        late = tile("late", 2 * I, BF16)
-        third_turned = psum.tile([P, 1, 2, P], F32, name="third_turned")
-        gather_vals(2, third_turned[:, 0])
-        interleave(late[:, I : 2 * I], third_turned)
 
-        recip = tile("recip", I, F32, "warm")
+        recip = tile("recip", I, F32)
         row_sum = tile("row_sum", 1, F32)
-        nc.vector.scalar_tensor_tensor(recip[:], magnitude[:], 1.0, signs[:], MULT, MULT, accum_out=row_sum[:])
-        early_mx = quantize(early, "early", 2 * P, "signs")
+        nc.vector.scalar_tensor_tensor(recip[:], positive[:], 0.5, magnitude[:], SUBTRACT, MULT, accum_out=row_sum[:])
+        early_mx = quantize(early, "early", 2 * P, "magnitude")
         inv_sum = tile("inv_sum", 1, F32)
         nc.vector.reciprocal(inv_sum[:], row_sum[:])
         weights = tile("weights", I, BF16)
@@ -169,25 +187,30 @@ def tile_attend_necread_kernel(tc, query, keys_words, keys_scales, kn, qn, size,
             MULT,
             MULT,
         )
-        weights_turned = psum.tile([P, 1, 2, P], F32, name="weights_turned")
+        late = tile("late", 2 * I, BF16)
+        weights_turned = psum.tile([P, 1, 2, P], F32, name="weights_turned", tag="scores0")
         turn(weights, weights_turned[:, 0])
         interleave(late[:, 0:I], weights_turned)
 
+        third_turned = psum.tile([P, 1, 2, P], F32, name="third_turned", tag="turn")
+        gather_vals(2, third_turned[:, 0], "recip")
+        interleave(late[:, I : 2 * I], third_turned)
+
         last = tile("last", I, BF16)
-        last_turned = psum.tile([P, 1, 2, P], F32, name="last_turned")
-        gather_vals(3, last_turned[:, 0], "warm")
+        last_turned = psum.tile([P, 1, 2, P], F32, name="last_turned", tag="part_rows1")
+        gather_vals(3, last_turned[:, 0])
         interleave(last[:], last_turned)
-        late_mx = quantize(late, "late", 2 * P, "word_pool")
+        late_mx = quantize(late, "late", 2 * P, "query_grouped")
         last_mx = quantize(last, "last", P)
 
         acc = psum.tile([P, 3 * P], F32, name="acc")
         multiply(acc[:, 0 : 2 * P], late_mx, 0, early_mx, 0, 2 * P)
         multiply(acc[:, 2 * P : 3 * P], late_mx, 0, late_mx, P, P)
         result = tile("result", 3 * P, F32)
-        nc.scalar.copy(result[:], acc[:])
+        nc.vector.tensor_copy(result[:], acc[:])
         nc.sync.dma_start(out[:, 0 : 3 * P], result[:])
 
-        acc_last = psum.tile([P, P], F32, name="acc_last", tag="part_rows")
+        acc_last = psum.tile([P, P], F32, name="acc_last")
         multiply(acc_last[:], late_mx, 0, last_mx, 0, P)
         result_last = tile("result_last", P, F32)
         nc.scalar.copy(result_last[:], acc_last[:])

@@ -21,9 +21,7 @@ FP8X4 = mybir.dt.float8_e4m3fn_x4
 ACT = mybir.ActivationFunctionType
 MULT = mybir.AluOpType.mult
 ADD = mybir.AluOpType.add
-SUBTRACT = mybir.AluOpType.subtract
 IS_EQUAL = mybir.AluOpType.is_equal
-IS_GE = mybir.AluOpType.is_ge
 
 
 def tile_attend_necread_kernel(tc, query, keys_words, keys_scales, kn, qn, size, vals, offs, out):
@@ -44,10 +42,14 @@ def tile_attend_necread_kernel(tc, query, keys_words, keys_scales, kn, qn, size,
         nc.vector.memset(kn_pool[:, 0:KN_SPLIT].bitcast(I32), 0)
         nc.gpsimd.memset(kn_pool[:, KN_SPLIT:T].bitcast(I32), 0)
 
+        zero = tile("zero", 1, F32)
+        nc.gpsimd.memset(zero[:], 0.0)
         diagonal = tile("diagonal", P, I32)
         nc.gpsimd.iota(diagonal[:], [[1, P]], base=0, channel_multiplier=-1)
+        one = tile("one", 1, F32)
+        nc.gpsimd.memset(one[:], 1.0)
         ident = tile("ident", P, F32)
-        nc.vector.tensor_scalar(ident[:], diagonal[:], 0.0, None, IS_EQUAL)
+        nc.vector.tensor_scalar(ident[:], diagonal[:], zero[:], None, IS_EQUAL)
 
         word_pool = tile("word_pool", T, I32)
         nc.sync.dma_start(word_pool[:], keys_words[0].rearrange("p n t -> p (n t)").bitcast(I32))
@@ -63,8 +65,8 @@ def tile_attend_necread_kernel(tc, query, keys_words, keys_scales, kn, qn, size,
                 keys_scales[0, 4 * quad : 4 * quad + 4, :].bitcast(I32),
             )
         nc.sync.dma_start(kn_pool[0:1, :], kn[0:1, :])
-        warm = tile("warm", 2, F32)
-        nc.scalar.activation(warm[64:128, :], kn_pool[64:128, KN_SPLIT - 1 : KN_SPLIT + 1], ACT.Abs_reciprocal_sqrt, bias=1.0)
+        query_grouped = tile("query_grouped", Q * PACK, BF16)
+        nc.scalar.activation(query_grouped[:, 0:1], ident[:, 0:1], ACT.Abs_reciprocal_sqrt, bias=one[:])
 
         row_bias = tile("row_bias", 1, F32)
         nc.gpsimd.tensor_scalar(row_bias[:], qn_col[:], 1.0, 0.1, MULT, ADD)
@@ -107,12 +109,11 @@ def tile_attend_necread_kernel(tc, query, keys_words, keys_scales, kn, qn, size,
             nc.vector.tensor_copy(listed[:], vals_pools[c][:].indirect(offsets[:]))
             turn(listed, bank)
 
-        query_grouped = tile("query_grouped", Q * PACK, BF16)
         nc.scalar.copy(
             query_grouped[:].rearrange("p (q j) -> p q j", j=PACK),
             query_raw[:].rearrange("p (j q) -> p q j", j=PACK),
         )
-        key_words = tile("key_words", I, U32)
+        key_words = tile("key_words", I, U32, "zero")
         nc.vector.tensor_copy(key_words[:], word_pool[:].bitcast(U32).indirect(offsets[:]))
         kn_listed = tile("kn_listed", I, F32, "word_pool")
         nc.vector.tensor_copy(kn_listed[:], kn_pool[:].indirect(offsets[:]))
@@ -125,7 +126,7 @@ def tile_attend_necread_kernel(tc, query, keys_words, keys_scales, kn, qn, size,
             )
 
         vals_pools = [
-            load_vals(c, after) for c, after in enumerate(("diagonal", "warm", "query_raw", "query_grouped"))
+            load_vals(c, after) for c, after in enumerate(("diagonal", "one", "query_raw", "query_grouped"))
         ]
 
         kn_turned = psum.tile([P, PACK, P], F32, name="kn_turned", tag="turn")
@@ -150,32 +151,32 @@ def tile_attend_necread_kernel(tc, query, keys_words, keys_scales, kn, qn, size,
                 nc.tensor.transpose(part_rows[h][:, jj * P : (jj + 1) * P], part[:, cols], ident[:])
 
         root = tile("root", I, F32)
+        signs = tile("signs", I, F32)
         magnitude = tile("magnitude", I, F32)
         for h in range(2):
             cols = slice(h * HALF, (h + 1) * HALF)
             nc.scalar.activation(root[:, cols], part_rows[h][:], ACT.Abs_reciprocal_sqrt, bias=row_bias[:])
+            nc.scalar.activation(signs[:, cols], part_rows[h][:], ACT.Sign, bias=row_bias[:])
             nc.scalar.activation(magnitude[:, cols], root[:, cols], ACT.Square)
-
-        early_turned = psum.tile([P, 2, 2, P], F32, name="early_turned", tag="scores1")
-        for c in range(2):
-            gather_vals(c, early_turned[:, c])
-        positive = tile("positive", I, F32, "warm")
-        for h in range(2):
-            nc.vector.tensor_scalar(
-                positive[:, h * HALF : (h + 1) * HALF], part_rows[h][:], row_bias[:], 0.0, ADD, IS_GE
-            )
 
         size_rows = psum.tile([P, PACK, P], F32, name="size_rows", tag="part_rows0")
         for t in range(PACK):
             nc.tensor.transpose(size_rows[:, t, :], size_cols[:, t : t + 1].to_broadcast([P, P]), ident[:])
 
         early = tile("early", 2 * I, BF16, "root")
+        early_turned = psum.tile([P, 2, 2, P], F32, name="early_turned", tag="scores1")
+        for c in range(2):
+            gather_vals(c, early_turned[:, c])
         interleave(early[:], early_turned)
+        late = tile("late", 2 * I, BF16)
+        third_turned = psum.tile([P, 1, 2, P], F32, name="third_turned", tag="turn")
+        gather_vals(2, third_turned[:, 0], "one")
+        interleave(late[:, I : 2 * I], third_turned)
 
-        recip = tile("recip", I, F32)
+        recip = tile("recip", I, F32, "query_raw")
         row_sum = tile("row_sum", 1, F32)
-        nc.vector.scalar_tensor_tensor(recip[:], positive[:], 0.5, magnitude[:], SUBTRACT, MULT, accum_out=row_sum[:])
-        early_mx = quantize(early, "early", 2 * P, "magnitude")
+        nc.vector.scalar_tensor_tensor(recip[:], magnitude[:], 1.0, signs[:], MULT, MULT, accum_out=row_sum[:])
+        early_mx = quantize(early, "early", 2 * P, "signs")
         inv_sum = tile("inv_sum", 1, F32)
         nc.vector.reciprocal(inv_sum[:], row_sum[:])
         weights = tile("weights", I, BF16)
@@ -187,18 +188,13 @@ def tile_attend_necread_kernel(tc, query, keys_words, keys_scales, kn, qn, size,
             MULT,
             MULT,
         )
-        late = tile("late", 2 * I, BF16)
         weights_turned = psum.tile([P, 1, 2, P], F32, name="weights_turned", tag="scores0")
         turn(weights, weights_turned[:, 0])
         interleave(late[:, 0:I], weights_turned)
 
-        third_turned = psum.tile([P, 1, 2, P], F32, name="third_turned", tag="turn")
-        gather_vals(2, third_turned[:, 0], "recip")
-        interleave(late[:, I : 2 * I], third_turned)
-
         last = tile("last", I, BF16)
         last_turned = psum.tile([P, 1, 2, P], F32, name="last_turned", tag="part_rows1")
-        gather_vals(3, last_turned[:, 0])
+        gather_vals(3, last_turned[:, 0], "query_raw")
         interleave(last[:], last_turned)
         late_mx = quantize(late, "late", 2 * P, "query_grouped")
         last_mx = quantize(last, "last", P)

@@ -5,6 +5,8 @@ import concourse.mybir as mybir
 D, T, I, Q, E = 512, 2048, 512, 128, 512
 P = 128
 PACK = 4
+LIST_ROWS = 16
+QUADRANT = 32
 HALF = I // 2
 KN_SPLIT = 1408
 
@@ -30,55 +32,15 @@ def tile_attend_necread_kernel(tc, query, keys_words, keys_scales, kn, qn, size,
         sbuf = ctx.enter_context(tc.tile_pool(name="sbuf", bufs=1))
         psum = ctx.enter_context(tc.psum_pool(name="psum", bufs=1))
 
-        def tile(name, columns, dtype, after=None):
-            return sbuf.tile([P, columns], dtype, name=name, tag=after or name, align_bytes=64)
+        def tile(name, columns, dtype, tag=None):
+            return sbuf.tile([P, columns], dtype, name=name, tag=tag or name, align_bytes=64)
 
-        offsets = tile("offsets", I // 16, U16)
-        nc.sync.dma_start(offsets[:], offs)
+        def bank(name, shape, tag=None):
+            return psum.tile([P] + shape, F32, name=name, tag=tag or name)
 
-        scale_pool = tile("scale_pool", T, U8)
-        nc.gpsimd.memset(scale_pool[:].bitcast(I32), 0)
-        kn_pool = tile("kn_pool", T, F32)
-        nc.vector.memset(kn_pool[:, 0:KN_SPLIT].bitcast(I32), 0)
-        nc.gpsimd.memset(kn_pool[:, KN_SPLIT:T].bitcast(I32), 0)
-
-        zero = tile("zero", 1, F32)
-        nc.gpsimd.memset(zero[:], 0.0)
-        diagonal = tile("diagonal", P, I32)
-        nc.gpsimd.iota(diagonal[:], [[1, P]], base=0, channel_multiplier=-1)
-        one = tile("one", 1, F32)
-        nc.gpsimd.memset(one[:], 1.0)
-        ident = tile("ident", P, F32)
-        nc.vector.tensor_scalar(ident[:], diagonal[:], zero[:], None, IS_EQUAL)
-
-        word_pool = tile("word_pool", T, I32)
-        nc.sync.dma_start(word_pool[:], keys_words[0].rearrange("p n t -> p (n t)").bitcast(I32))
-        query_raw = tile("query_raw", PACK * Q, F32)
-        nc.sync.dma_start(query_raw[:], query.rearrange("(p j) q -> p (j q)", j=PACK))
-        qn_col = tile("qn_col", 1, F32)
-        nc.gpsimd.dma_start(qn_col[:], qn)
-        size_cols = tile("size_cols", PACK, F32)
-        nc.gpsimd.dma_start(size_cols[:], size.rearrange("o (p t) -> (o p) t", t=PACK))
-        for quad in range(4):
-            nc.sync.dma_start(
-                scale_pool[32 * quad : 32 * quad + 4, :].bitcast(I32),
-                keys_scales[0, 4 * quad : 4 * quad + 4, :].bitcast(I32),
-            )
-        nc.sync.dma_start(kn_pool[0:1, :], kn[0:1, :])
-        query_grouped = tile("query_grouped", Q * PACK, BF16)
-        nc.scalar.activation(query_grouped[:, 0:1], ident[:, 0:1], ACT.Abs_reciprocal_sqrt, bias=one[:])
-
-        row_bias = tile("row_bias", 1, F32)
-        nc.gpsimd.tensor_scalar(row_bias[:], qn_col[:], 1.0, 0.1, MULT, ADD)
-
-        def load_vals(c, after):
-            pool_c = tile(f"vals{c}", T, F32, after)
-            nc.sync.dma_start(pool_c[:], vals[c * P : (c + 1) * P, :])
-            return pool_c
-
-        def quantize(grouped, name, words, after=None):
-            codes = tile(name + "_codes", words, U32, after)
-            scales = tile(name + "_scales", words, U8)
+        def quantize(grouped, name, columns, tag=None):
+            codes = tile(name + "_codes", columns, U32, tag)
+            scales = tile(name + "_scales", columns, U8)
             nc.vector.quantize_mx(out=codes[:].bitcast(FP8X4), scales=scales[:], in_=grouped[:])
             return codes, scales
 
@@ -93,90 +55,135 @@ def tile_attend_necread_kernel(tc, query, keys_words, keys_scales, kn, qn, size,
                 stop=True,
             )
 
-        def turn(rows, bank):
+        def turn(rows, turned):
             words = rows[:].bitcast(F32)
             for u in range(2):
-                nc.tensor.transpose(bank[:, u, :], words[:, u : I // 2 : 2], ident[:])
+                nc.tensor.transpose(turned[:, u, :], words[:, u : I // 2 : 2], ident[:])
 
-        def interleave(grouped, bank):
+        def interleave(grouped, turned):
             nc.scalar.copy(
                 grouped.bitcast(F32).rearrange("p (c r u) -> p c r u", r=P, u=2),
-                bank[:].rearrange("p c u r -> p c r u"),
+                turned[:].rearrange("p c u r -> p c r u"),
             )
 
-        def gather_vals(c, bank, after=None):
-            listed = tile(f"listed{c}", I, BF16, after)
+        def gather_vals(c, turned, tag):
+            listed = tile(f"listed{c}", I, BF16, tag)
             nc.vector.tensor_copy(listed[:], vals_pools[c][:].indirect(offsets[:]))
-            turn(listed, bank)
+            turn(listed, turned)
 
-        nc.scalar.copy(
-            query_grouped[:].rearrange("p (q j) -> p q j", j=PACK),
-            query_raw[:].rearrange("p (j q) -> p q j", j=PACK),
-        )
+        offsets = tile("offsets", I // LIST_ROWS, U16)
+        nc.sync.dma_start(offsets[:], offs)
+
+        scale_pool = tile("scale_pool", T, U8)
+        nc.gpsimd.memset(scale_pool[:].bitcast(I32), 0)
+        kn_pool = tile("kn_pool", T, F32)
+        nc.vector.memset(kn_pool[:, 0:KN_SPLIT].bitcast(I32), 0)
+        nc.gpsimd.memset(kn_pool[:, KN_SPLIT:T].bitcast(I32), 0)
+
+        zero = tile("zero", 1, F32)
+        nc.gpsimd.memset(zero[:], 0.0)
+        ident = tile("ident", P, F32)
+        for part_index in range(2):
+            first = part_index * P // 2
+            distance = tile(f"distance{part_index}", P // 2, I32)
+            nc.gpsimd.iota(distance[:], [[1, P // 2]], base=first, channel_multiplier=-1)
+            nc.vector.tensor_scalar(ident[:, first : first + P // 2], distance[:], zero[:], None, IS_EQUAL)
+        one = tile("one", 1, F32)
+        nc.gpsimd.memset(one[:], 1.0)
+
+        word_pool = tile("word_pool", T, I32)
+        nc.sync.dma_start(word_pool[:], keys_words[0].rearrange("p n t -> p (n t)").bitcast(I32))
+        query_raw = tile("query_raw", PACK * Q, F32)
+        nc.sync.dma_start(query_raw[:], query.rearrange("(p t) q -> p (t q)", t=PACK))
+        qn_col = tile("qn_col", 1, F32)
+        nc.gpsimd.dma_start(qn_col[:], qn)
+        size_cols = tile("size_cols", PACK, F32)
+        nc.gpsimd.dma_start(size_cols[:], size.rearrange("o (p t) -> (o p) t", t=PACK))
+        for quad in range(P // QUADRANT):
+            nc.sync.dma_start(
+                scale_pool[QUADRANT * quad : QUADRANT * quad + 4, :].bitcast(I32),
+                keys_scales[0, 4 * quad : 4 * quad + 4, :].bitcast(I32),
+            )
+        nc.sync.dma_start(kn_pool[0:1, :], kn[0:1, :])
+
+        row_factor = tile("row_factor", 1, F32)
+        nc.scalar.activation(row_factor[:], ident[:, P - 1 : P], ACT.Abs_reciprocal_sqrt, bias=one[:])
+
+        row_bias = tile("row_bias", 1, F32)
+        nc.gpsimd.tensor_scalar(row_bias[:], qn_col[:], 1.0, 0.1, MULT, ADD)
+
         key_words = tile("key_words", I, U32, "zero")
         nc.vector.tensor_copy(key_words[:], word_pool[:].bitcast(U32).indirect(offsets[:]))
-        kn_listed = tile("kn_listed", I, F32, "word_pool")
+        query_grouped = tile("query_grouped", Q * PACK, BF16, "one")
+        nc.scalar.copy(
+            query_grouped[:].rearrange("p (q t) -> p q t", t=PACK),
+            query_raw[:].rearrange("p (t q) -> p q t", t=PACK),
+        )
+        query_mx = quantize(query_grouped, "query", Q, "word_pool")
+        kn_listed = tile("kn_listed", I, F32, "one")
         nc.vector.tensor_copy(kn_listed[:], kn_pool[:].indirect(offsets[:]))
         key_scales = tile("key_scales", I, U8, "kn_pool")
-        query_mx = quantize(query_grouped, "query", Q)
         for h in range(2):
             nc.vector.tensor_copy(
                 key_scales[:, h * HALF : (h + 1) * HALF],
-                scale_pool[:].indirect(offsets[:, h * HALF // 16 : (h + 1) * HALF // 16]),
+                scale_pool[:].indirect(offsets[:, h * HALF // LIST_ROWS : (h + 1) * HALF // LIST_ROWS]),
             )
 
-        vals_pools = [
-            load_vals(c, after) for c, after in enumerate(("diagonal", "one", "query_raw", "query_grouped"))
-        ]
-
-        kn_turned = psum.tile([P, PACK, P], F32, name="kn_turned", tag="turn")
+        kn_turned = bank("kn_turned", [PACK, P])
         for j in range(PACK):
             nc.tensor.transpose(kn_turned[:, j, :], kn_listed[:, j * P : (j + 1) * P], ident[:])
         kn_cols = tile("kn_cols", PACK, F32)
         nc.scalar.copy(kn_cols[:], kn_turned[:, :, 0])
 
-        part = tile("part", PACK * Q, F32)
-        part_rows = []
+        vals_pools = []
+        for c, tag in enumerate(("distance0", "distance1", "query_raw", "one")):
+            vals_pools.append(tile(f"vals{c}", T, F32, tag))
+            nc.sync.dma_start(vals_pools[c][:], vals[c * P : (c + 1) * P, :])
+
+        partial = tile("partial", PACK * Q, F32)
+        partial_rows = []
         for h in range(2):
-            scores = psum.tile([P, 2, Q], F32, name=f"scores{h}")
+            scores = bank(f"scores{h}", [2, Q])
             for jj in range(2):
                 multiply(scores[:, jj, :], (key_words, key_scales), (2 * h + jj) * P, query_mx, 0, Q)
-            part_rows.append(psum.tile([P, HALF], F32, name=f"part_rows{h}"))
+            partial_rows.append(bank(f"partial_rows{h}", [HALF]))
             for jj in range(2):
                 j = 2 * h + jj
                 cols = slice(j * P, (j + 1) * P)
                 nc.scalar.activation(
-                    part[:, cols], scores[:, jj, :], ACT.Identity, bias=kn_cols[:, j : j + 1], scale=-2.0
+                    partial[:, cols], scores[:, jj, :], ACT.Identity, bias=kn_cols[:, j : j + 1], scale=-2.0
                 )
-                nc.tensor.transpose(part_rows[h][:, jj * P : (jj + 1) * P], part[:, cols], ident[:])
+                nc.tensor.transpose(partial_rows[h][:, jj * P : (jj + 1) * P], partial[:, cols], ident[:])
 
         root = tile("root", I, F32)
         signs = tile("signs", I, F32)
         magnitude = tile("magnitude", I, F32)
         for h in range(2):
             cols = slice(h * HALF, (h + 1) * HALF)
-            nc.scalar.activation(root[:, cols], part_rows[h][:], ACT.Abs_reciprocal_sqrt, bias=row_bias[:])
-            nc.scalar.activation(signs[:, cols], part_rows[h][:], ACT.Sign, bias=row_bias[:])
+            nc.scalar.activation(root[:, cols], partial_rows[h][:], ACT.Abs_reciprocal_sqrt, bias=row_bias[:])
+            nc.scalar.activation(signs[:, cols], partial_rows[h][:], ACT.Sign, bias=row_bias[:])
             nc.scalar.activation(magnitude[:, cols], root[:, cols], ACT.Square)
 
-        size_rows = psum.tile([P, PACK, P], F32, name="size_rows", tag="part_rows0")
+        size_rows = bank("size_rows", [PACK, P], "partial_rows1")
         for t in range(PACK):
             nc.tensor.transpose(size_rows[:, t, :], size_cols[:, t : t + 1].to_broadcast([P, P]), ident[:])
 
-        early = tile("early", 2 * I, BF16, "root")
-        early_turned = psum.tile([P, 2, 2, P], F32, name="early_turned", tag="scores1")
-        for c in range(2):
-            gather_vals(c, early_turned[:, c])
-        interleave(early[:], early_turned)
-        late = tile("late", 2 * I, BF16)
-        third_turned = psum.tile([P, 1, 2, P], F32, name="third_turned", tag="turn")
-        gather_vals(2, third_turned[:, 0], "one")
-        interleave(late[:, I : 2 * I], third_turned)
+        first_two = tile("first_two", 2 * I, BF16, "root")
+        first_two_turned = bank("first_two_turned", [2, 2, P], "scores1")
+        gather_vals(0, first_two_turned[:, 0], "scale_pool")
+        gather_vals(1, first_two_turned[:, 1], "distance0")
+        interleave(first_two[:], first_two_turned)
+        weights_and_third = tile("weights_and_third", 2 * I, BF16)
+        third_turned = bank("third_turned", [1, 2, P], "scores1")
+        gather_vals(2, third_turned[:, 0], "distance1")
+        interleave(weights_and_third[:, I : 2 * I], third_turned)
 
         recip = tile("recip", I, F32, "query_raw")
         row_sum = tile("row_sum", 1, F32)
-        nc.vector.scalar_tensor_tensor(recip[:], magnitude[:], 1.0, signs[:], MULT, MULT, accum_out=row_sum[:])
-        early_mx = quantize(early, "early", 2 * P, "signs")
+        nc.vector.scalar_tensor_tensor(
+            recip[:], magnitude[:], row_factor[:], signs[:], MULT, MULT, accum_out=row_sum[:]
+        )
+        first_two_mx = quantize(first_two, "first_two", 2 * P, "signs")
         inv_sum = tile("inv_sum", 1, F32)
         nc.vector.reciprocal(inv_sum[:], row_sum[:])
         weights = tile("weights", I, BF16)
@@ -188,26 +195,26 @@ def tile_attend_necread_kernel(tc, query, keys_words, keys_scales, kn, qn, size,
             MULT,
             MULT,
         )
-        weights_turned = psum.tile([P, 1, 2, P], F32, name="weights_turned", tag="scores0")
+        weights_turned = bank("weights_turned", [1, 2, P], "scores0")
         turn(weights, weights_turned[:, 0])
-        interleave(late[:, 0:I], weights_turned)
+        interleave(weights_and_third[:, 0:I], weights_turned)
 
         last = tile("last", I, BF16)
-        last_turned = psum.tile([P, 1, 2, P], F32, name="last_turned", tag="part_rows1")
+        last_turned = bank("last_turned", [1, 2, P], "partial_rows0")
         gather_vals(3, last_turned[:, 0], "query_raw")
         interleave(last[:], last_turned)
-        late_mx = quantize(late, "late", 2 * P, "query_grouped")
+        weights_and_third_mx = quantize(weights_and_third, "weights_and_third", 2 * P, "one")
         last_mx = quantize(last, "last", P)
 
-        acc = psum.tile([P, 3 * P], F32, name="acc")
-        multiply(acc[:, 0 : 2 * P], late_mx, 0, early_mx, 0, 2 * P)
-        multiply(acc[:, 2 * P : 3 * P], late_mx, 0, late_mx, P, P)
-        result = tile("result", 3 * P, F32)
+        acc = bank("acc", [3 * P])
+        multiply(acc[:, 0 : 2 * P], weights_and_third_mx, 0, first_two_mx, 0, 2 * P)
+        multiply(acc[:, 2 * P : 3 * P], weights_and_third_mx, 0, weights_and_third_mx, P, P)
+        result = tile("result", 3 * P, F32, "last")
         nc.vector.tensor_copy(result[:], acc[:])
         nc.sync.dma_start(out[:, 0 : 3 * P], result[:])
 
-        acc_last = psum.tile([P, P], F32, name="acc_last")
-        multiply(acc_last[:], late_mx, 0, last_mx, 0, P)
+        acc_last = bank("acc_last", [P])
+        multiply(acc_last[:], weights_and_third_mx, 0, last_mx, 0, P)
         result_last = tile("result_last", P, F32)
         nc.scalar.copy(result_last[:], acc_last[:])
         nc.scalar.dma_start(out[:, 3 * P : E], result_last[:])

from contextlib import ExitStack

import concourse.mybir as mybir

D, T, I, Q, E = 512, 2048, 512, 128, 512
P = 128
PACK = 4
LIST_ROWS = 16
QUADRANT = 32
HALF = I // 2
KN_SPLIT = 1408

FLOPS = 2 * Q * I * D + 2 * Q * I * E
BYTES = 4 * D * Q + D * T + (D // 32) * T + 4 * T + 4 * Q + 4 * I + 4 * E * T + 2 * P * (I // 16) + 4 * Q * E

F32 = mybir.dt.float32
BF16 = mybir.dt.bfloat16
I32 = mybir.dt.int32
U32 = mybir.dt.uint32
U16 = mybir.dt.uint16
U8 = mybir.dt.uint8
FP8X4 = mybir.dt.float8_e4m3fn_x4
ACT = mybir.ActivationFunctionType
MULT = mybir.AluOpType.mult
ADD = mybir.AluOpType.add
IS_EQUAL = mybir.AluOpType.is_equal


def tile_attend_necread_kernel(tc, query, keys_words, keys_scales, kn, qn, size, vals, offs, out):
    nc = tc.nc
    with ExitStack() as ctx:
        sbuf = ctx.enter_context(tc.tile_pool(name="sbuf", bufs=1))
        psum = ctx.enter_context(tc.psum_pool(name="psum", bufs=1))

        def tile(name, columns, dtype, tag=None):
            return sbuf.tile([P, columns], dtype, name=name, tag=tag or name, align_bytes=64)

        def bank(name, shape, tag=None):
            return psum.tile([P] + shape, F32, name=name, tag=tag or name)

        def quantize(grouped, name, columns, tag=None):
            codes = tile(name + "_codes", columns, U32, tag)
            scales = tile(name + "_scales", columns, U8)
            nc.vector.quantize_mx(out=codes[:].bitcast(FP8X4), scales=scales[:], in_=grouped[:])
            return codes, scales

        def multiply(acc, lhs, lhs_first, rhs, rhs_first, columns):
            nc.tensor.matmul_mx(
                out=acc,
                lhsT=lhs[0][:, lhs_first : lhs_first + P].bitcast(FP8X4),
                lhsT_scale=lhs[1][:, lhs_first : lhs_first + P],
                rhs=rhs[0][:, rhs_first : rhs_first + columns].bitcast(FP8X4),
                rhs_scale=rhs[1][:, rhs_first : rhs_first + columns],
                start=True,
                stop=True,
            )

        def turn(rows, turned):
            words = rows[:].bitcast(F32)
            for u in range(2):
                nc.tensor.transpose(turned[:, u, :], words[:, u : I // 2 : 2], ident[:])

        def interleave(grouped, turned):
            nc.scalar.copy(
                grouped.bitcast(F32).rearrange("p (c r u) -> p c r u", r=P, u=2),
                turned[:].rearrange("p c u r -> p c r u"),
            )

        def gather_vals(c, turned, tag):
            listed = tile(f"listed{c}", I, BF16, tag)
            nc.vector.tensor_copy(listed[:], vals_pools[c][:].indirect(offsets[:]))
            turn(listed, turned)

        offsets = tile("offsets", I // LIST_ROWS, U16)
        nc.sync.dma_start(offsets[:], offs)

        scale_pool = tile("scale_pool", T, U8)
        nc.gpsimd.memset(scale_pool[:].bitcast(I32), 0)
        kn_pool = tile("kn_pool", T, F32)
        nc.vector.memset(kn_pool[:, 0:KN_SPLIT].bitcast(I32), 0)
        nc.gpsimd.memset(kn_pool[:, KN_SPLIT:T].bitcast(I32), 0)

        zero = tile("zero", 1, F32)
        nc.gpsimd.memset(zero[:], 0.0)
        ident = tile("ident", P, F32)
        for part_index in range(2):
            first = part_index * P // 2
            distance = tile(f"distance{part_index}", P // 2, I32)
            nc.gpsimd.iota(distance[:], [[1, P // 2]], base=first, channel_multiplier=-1)
            nc.vector.tensor_scalar(ident[:, first : first + P // 2], distance[:], zero[:], None, IS_EQUAL)
        one = tile("one", 1, F32)
        nc.gpsimd.memset(one[:], 1.0)

        word_pool = tile("word_pool", T, I32)
        nc.sync.dma_start(word_pool[:], keys_words[0].rearrange("p n t -> p (n t)").bitcast(I32))
        query_raw = tile("query_raw", PACK * Q, F32)
        nc.sync.dma_start(query_raw[:], query.rearrange("(p t) q -> p (t q)", t=PACK))
        qn_col = tile("qn_col", 1, F32)
        nc.gpsimd.dma_start(qn_col[:], qn)
        size_cols = tile("size_cols", PACK, F32)
        nc.gpsimd.dma_start(size_cols[:], size.rearrange("o (p t) -> (o p) t", t=PACK))
        for quad in range(P // QUADRANT):
            nc.sync.dma_start(
                scale_pool[QUADRANT * quad : QUADRANT * quad + 4, :].bitcast(I32),
                keys_scales[0, 4 * quad : 4 * quad + 4, :].bitcast(I32),
            )
        nc.sync.dma_start(kn_pool[0:1, :], kn[0:1, :])

        row_factor = tile("row_factor", 1, F32)
        nc.scalar.activation(row_factor[:], ident[:, P - 1 : P], ACT.Abs_reciprocal_sqrt, bias=one[:])

        row_bias = tile("row_bias", 1, F32)
        nc.gpsimd.tensor_scalar(row_bias[:], qn_col[:], 1.0, 0.1, MULT, ADD)

        key_words = tile("key_words", I, U32, "zero")
        nc.vector.tensor_copy(key_words[:], word_pool[:].bitcast(U32).indirect(offsets[:]))
        query_grouped = tile("query_grouped", Q * PACK, BF16, "one")
        nc.scalar.copy(
            query_grouped[:].rearrange("p (q t) -> p q t", t=PACK),
            query_raw[:].rearrange("p (t q) -> p q t", t=PACK),
        )
        query_mx = quantize(query_grouped, "query", Q, "word_pool")
        kn_listed = tile("kn_listed", I, F32, "one")
        nc.vector.tensor_copy(kn_listed[:], kn_pool[:].indirect(offsets[:]))
        key_scales = tile("key_scales", I, U8, "kn_pool")
        for h in range(2):
            nc.vector.tensor_copy(
                key_scales[:, h * HALF : (h + 1) * HALF],
                scale_pool[:].indirect(offsets[:, h * HALF // LIST_ROWS : (h + 1) * HALF // LIST_ROWS]),
            )

        kn_turned = bank("kn_turned", [PACK, P])
        for j in range(PACK):
            nc.tensor.transpose(kn_turned[:, j, :], kn_listed[:, j * P : (j + 1) * P], ident[:])
        kn_cols = tile("kn_cols", PACK, F32)
        nc.scalar.copy(kn_cols[:], kn_turned[:, :, 0])

        vals_pools = []
        for c, tag in enumerate(("distance0", "distance1", "query_raw", "one")):
            vals_pools.append(tile(f"vals{c}", T, F32, tag))
            nc.sync.dma_start(vals_pools[c][:], vals[c * P : (c + 1) * P, :])

        partial = tile("partial", PACK * Q, F32)
        partial_rows = []
        for h in range(2):
            scores = bank(f"scores{h}", [2, Q])
            for jj in range(2):
                multiply(scores[:, jj, :], (key_words, key_scales), (2 * h + jj) * P, query_mx, 0, Q)
            partial_rows.append(bank(f"partial_rows{h}", [HALF]))
            for jj in range(2):
                j = 2 * h + jj
                cols = slice(j * P, (j + 1) * P)
                nc.scalar.activation(
                    partial[:, cols], scores[:, jj, :], ACT.Identity, bias=kn_cols[:, j : j + 1], scale=-2.0
                )
                nc.tensor.transpose(partial_rows[h][:, jj * P : (jj + 1) * P], partial[:, cols], ident[:])

        root = tile("root", I, F32)
        signs = tile("signs", I, F32)
        magnitude = tile("magnitude", I, F32)
        for h in range(2):
            cols = slice(h * HALF, (h + 1) * HALF)
            nc.scalar.activation(root[:, cols], partial_rows[h][:], ACT.Abs_reciprocal_sqrt, bias=row_bias[:])
            nc.scalar.activation(signs[:, cols], partial_rows[h][:], ACT.Sign, bias=row_bias[:])
            nc.scalar.activation(magnitude[:, cols], root[:, cols], ACT.Square)

        size_rows = bank("size_rows", [PACK, P], "partial_rows1")
        for t in range(PACK):
            nc.tensor.transpose(size_rows[:, t, :], size_cols[:, t : t + 1].to_broadcast([P, P]), ident[:])

        first_two = tile("first_two", 2 * I, BF16, "root")
        first_two_turned = bank("first_two_turned", [2, 2, P], "scores1")
        gather_vals(0, first_two_turned[:, 0], "scale_pool")
        gather_vals(1, first_two_turned[:, 1], "distance0")
        interleave(first_two[:], first_two_turned)
        weights_and_third = tile("weights_and_third", 2 * I, BF16)
        third_turned = bank("third_turned", [1, 2, P], "scores1")
        gather_vals(2, third_turned[:, 0], "distance1")
        interleave(weights_and_third[:, I : 2 * I], third_turned)

        recip = tile("recip", I, F32, "query_raw")
        row_sum = tile("row_sum", 1, F32)
        nc.vector.scalar_tensor_tensor(
            recip[:], magnitude[:], row_factor[:], signs[:], MULT, MULT, accum_out=row_sum[:]
        )
        first_two_mx = quantize(first_two, "first_two", 2 * P, "signs")
        inv_sum = tile("inv_sum", 1, F32)
        nc.vector.reciprocal(inv_sum[:], row_sum[:])
        weights = tile("weights", I, BF16)
        nc.vector.scalar_tensor_tensor(
            weights[:].rearrange("q (s t) -> q s t", t=PACK),
            recip[:].rearrange("q (s t) -> q s t", t=PACK),
            inv_sum[:],
            size_rows[:].rearrange("q t s -> q s t"),
            MULT,
            MULT,
        )
        weights_turned = bank("weights_turned", [1, 2, P], "scores0")
        turn(weights, weights_turned[:, 0])
        interleave(weights_and_third[:, 0:I], weights_turned)

        last = tile("last", I, BF16)
        last_turned = bank("last_turned", [1, 2, P], "partial_rows0")
        gather_vals(3, last_turned[:, 0], "query_raw")
        interleave(last[:], last_turned)
        weights_and_third_mx = quantize(weights_and_third, "weights_and_third", 2 * P, "one")
        last_mx = quantize(last, "last", P)

        acc = bank("acc", [3 * P])
        multiply(acc[:, 0 : 2 * P], weights_and_third_mx, 0, first_two_mx, 0, 2 * P)
        multiply(acc[:, 2 * P : 3 * P], weights_and_third_mx, 0, weights_and_third_mx, P, P)
        result = tile("result", 3 * P, F32, "last")
        nc.vector.tensor_copy(result[:], acc[:])
        nc.sync.dma_start(out[:, 0 : 3 * P], result[:])

        acc_last = bank("acc_last", [P])
        multiply(acc_last[:], weights_and_third_mx, 0, last_mx, 0, P)
        result_last = tile("result_last", P, F32)
        nc.scalar.copy(result_last[:], acc_last[:])
        nc.scalar.dma_start(out[:, 3 * P : E], result_last[:])
